import numpy as np
import ml_dtypes


def mxq(x, axis, fmt="e4m3"):
    dtype, down = {"e4m3": (ml_dtypes.float8_e4m3fn, 7), "e5m2": (ml_dtypes.float8_e5m2, 14)}[fmt]
    v = np.moveaxis(np.asarray(x, np.float32).astype(ml_dtypes.bfloat16).astype(np.float64), axis, -1)
    blocks = v.reshape(v.shape[:-1] + (-1, 32))
    amax = np.abs(blocks).max(-1, keepdims=True)
    byte = np.maximum(np.where(amax > 0, np.frexp(amax)[1] - 1 + 127, 0) - down, 1)
    scale = np.exp2(byte - 127.0)
    codes = (blocks / scale).astype(np.float32).astype(dtype).astype(np.float64)
    return np.moveaxis((codes * scale).reshape(v.shape), -1, axis)


WIDE = False


def mx_kscale(k):
    if not WIDE:
        return np.ones(k)
    levels = np.array([10, -10, 5, -5, 0])
    if k % 512:
        return np.exp2(np.random.permutation(np.resize(levels, k // 32))).repeat(32)
    a = np.empty((k // 512, 16))
    for p in range(k // 512):
        a[p, :8] = np.random.permutation(np.resize(levels, 8))
        for g in range(8):
            far = levels[np.abs(levels - a[p, g]) >= 10]
            a[p, g + 8] = far[np.random.randint(len(far))]
    return np.exp2(a.ravel()).repeat(32)


def f64(x):
    return np.asarray(x).astype(np.float64)


def striped(idx):
    return np.tile(idx.reshape(-1, 16).T, (8, 1)).astype(np.uint16)


def unstriped(offs):
    return offs[:16].T.reshape(-1).astype(np.int64)


E2M1 = np.array([0.0, 0.5, 1.0, 1.5, 2.0, 3.0, 4.0, 6.0, -0.0, -0.5, -1.0, -1.5, -2.0, -3.0, -4.0, -6.0])


def pack_weight(w, fmt):
    k, n = w.shape
    w = f64(np.asarray(w, np.float32).astype(ml_dtypes.bfloat16)).reshape(k // 32, 32, n)
    amax = np.abs(w).max(1)
    if fmt == "e4m3":
        byte = np.frexp(amax)[1] - 1 + 127 - 7
    else:
        mant, ex = np.frexp(amax / 6.0)
        byte = np.where(mant > 0.5, ex, ex - 1) + 127
    byte = np.clip(np.where(amax > 0, byte, 1), 1, 254)
    scaled = (w * np.exp2(127.0 - byte)[:, None, :]).reshape(k, n).astype(np.float32)
    by_word = np.ascontiguousarray(scaled.reshape(k // 512, 128, 4, n).transpose(0, 1, 3, 2))
    if fmt == "e4m3":
        words = by_word.astype(ml_dtypes.float8_e4m3fn).view(np.uint8)
    else:
        c = by_word.astype(ml_dtypes.float4_e2m1fn).view(np.uint8) & 0xF
        words = (c[..., 0::2] | (c[..., 1::2] << 4)).reshape(k // 512, 128, 2 * n)
    return np.ascontiguousarray(words), np.ascontiguousarray(byte.astype(np.uint8).reshape(k // 512, 16, n))


def unpack_weight(words, scales, fmt):
    g, _, n = scales.shape
    words = np.ascontiguousarray(words).reshape(g, 128, n, -1)
    if fmt == "e4m3":
        vals = words.view(ml_dtypes.float8_e4m3fn).astype(np.float64)
    else:
        nib = np.empty((g, 128, n, 4), np.uint8)
        nib[..., 0::2] = words & 0xF
        nib[..., 1::2] = words >> 4
        vals = E2M1[nib]
    vals = vals * np.repeat(np.exp2(scales.astype(np.float64) - 127.0), 8, axis=1)[..., None]
    return vals.transpose(0, 1, 3, 2).reshape(g * 512, n)


def gelu(v):
    return 0.5 * v * (1.0 + np.tanh(np.sqrt(2.0 / np.pi) * (v + 0.044715 * v**3)))


def bf(x):
    return np.asarray(x, np.float32).astype(ml_dtypes.bfloat16)


def planes(Y):
    n, m = Y.shape
    b = f64(bf(Y)).reshape(n // 32, 32, m)
    amax = np.abs(b).max(1)
    byte = np.clip(np.where(amax > 0, np.frexp(amax)[1] - 1 + 127 - 7, 1), 1, 254)
    codes = (b * np.exp2(127.0 - byte)[:, None, :]).reshape(n, m).astype(np.float32).astype(ml_dtypes.float8_e4m3fn).view(np.uint8)
    words = codes.reshape(n // 512, 128, 4, m).transpose(0, 1, 3, 2)
    return np.ascontiguousarray(words), np.ascontiguousarray(byte.astype(np.uint8).reshape(n // 512, 16, m))


K, T, S, P, H, N = 1024, 2048, 1024, 512, 1024, 512

def setup_inputs():
    n = np.random.standard_normal
    s = mx_kscale(K)[:, None]
    u = mx_kscale(H)[:, None]
    tab_words, tab_scales = pack_weight(n((K, T)) * s, "e4m3")
    offs = striped(np.random.permutation(T)[:S])
    pos1 = striped(np.random.permutation(S)[:P])
    pos2 = striped(np.random.permutation(S)[:P])
    w1 = (n((K, H)) / np.sqrt(K) / s).astype(np.float32)
    cen = (0.6 * n(H)).astype(np.float32)
    gain = (np.random.uniform(0.5, 1.2, H) * u[:, 0]).astype(np.float32)
    w2_words, w2_scales = pack_weight(0.8 * n((K, H)) / np.sqrt(K) / s * u.T, "e2m1")
    wa = (0.65 * n((H, N)) / np.sqrt(H) / u).astype(np.float32)
    wb_words, wb_scales = pack_weight(n((H, N)) / np.sqrt(H) / u * np.exp(0.8 * n(N))[None, :], "e4m3")
    temp = np.random.uniform(0.4, 1.6, N).astype(np.float32)
    mix = (3.0 * n((N, P))).astype(np.float32)
    return {"tab_words": tab_words, "tab_scales": tab_scales, "offs": offs, "pos1": pos1, "pos2": pos2,
            "w1": w1, "cen": cen, "gain": gain, "w2_words": w2_words, "w2_scales": w2_scales,
            "wa": wa, "wb_words": wb_words, "wb_scales": wb_scales, "temp": temp, "mix": mix}

def reference(tab_words, tab_scales, offs, pos1, pos2, w1, cen, gain, w2_words, w2_scales,
              wa, wb_words, wb_scales, temp, mix):
    v = unpack_weight(tab_words, tab_scales, "e4m3")[:, unstriped(offs)]
    away = np.abs((mxq(f64(w1), 0, "e4m3").T @ v) - f64(cen)[:, None])
    h = f64(gain)[:, None] * away + (unpack_weight(w2_words, w2_scales, "e2m1").T @ v)
    hq = mxq(h, 0, "e4m3")
    e = mxq(f64(wa), 0, "e4m3").T @ hq
    d = unpack_weight(wb_words, wb_scales, "e4m3").T @ hq
    top = e.max(axis=1)
    a = np.exp(f64(temp)[:, None] * (e[:, unstriped(pos1)] - top[:, None]))
    y = f64(mix) * a * d[:, unstriped(pos2)]
    words, scales = planes(y)
    return y, words, scales

@@ -1,0 +1,307 @@
+from contextlib import ExitStack
+
+import concourse.mybir as mybir
+
+K, T, S, NPICK, H, N = 1024, 2048, 1024, 512, 1024, 512
+FLOPS = 2 * (2 * K * H * S + 2 * H * N * S)
+
+F32 = mybir.dt.float32
+BF16 = mybir.dt.bfloat16
+I32 = mybir.dt.int32
+U32 = mybir.dt.uint32
+U16 = mybir.dt.uint16
+U8 = mybir.dt.uint8
+FP8X4 = mybir.dt.float8_e4m3fn_x4
+FP4X4 = mybir.dt.float4_e2m1fn_x4
+ALU = mybir.AluOpType
+ACT = mybir.ActivationFunctionType
+
+P = 128
+PACK = 4
+PASS = P * PACK
+QUADS = 4
+LIST_GROUP = 16
+
+
+def tile_list_streak_linkage_features_kernel(
+    tc, tab_words, tab_scales, offs, pos1, pos2, w1, cen, gain, w2_words, w2_scales,
+    wa, wb_words, wb_scales, temp, mix, out_0, out_1, out_2,
+):
+    nc = tc.nc
+
+    def copy_on(engine, out, in_):
+        if engine == "scalar":
+            nc.scalar.copy(out=out, in_=in_)
+        else:
+            nc.vector.tensor_copy(out=out, in_=in_)
+
+    with ExitStack() as ctx:
+        keep = ctx.enter_context(tc.tile_pool(name="keep", bufs=1))
+        ring = ctx.enter_context(tc.tile_pool(name="ring", bufs=2))
+        psum = ctx.enter_context(tc.psum_pool(name="psum", bufs=8))
+
+        offs_sb = keep.tile([P, S // LIST_GROUP], U16, name="offs_sb")
+        pos1_sb = keep.tile([P, NPICK // LIST_GROUP], U16, name="pos1_sb")
+        pos2_sb = keep.tile([P, NPICK // LIST_GROUP], U16, name="pos2_sb")
+        tab_w = [keep.tile([P, T], U32, name="tab_w%d" % a, align_bytes=64) for a in range(2)]
+        tab_s = keep.tile([P, 2 * T], U8, name="tab_s", align_bytes=64)
+        w2_raw = keep.tile([P, 2 * H], U16, name="w2_raw", align_bytes=64)
+        w2s_raw = keep.tile([P, 2 * H], U8, name="w2s_raw", align_bytes=64)
+        wb_raw = keep.tile([P, 2 * N], U32, name="wb_raw", align_bytes=64)
+        w1_raw = {(a, b): keep.tile([P, PACK, PASS], F32, name="w1_raw%d%d" % (a, b)) for a in range(2) for b in range(2)}
+        wa_raw = [keep.tile([P, PACK, N], F32, name="wa_raw%d" % a) for a in range(2)]
+        cen_sb = keep.tile([P, 2, PACK], F32, name="cen_sb")
+        gain_sb = keep.tile([P, 2, PACK], F32, name="gain_sb")
+        temp_sb = keep.tile([P, PACK], F32, name="temp_sb")
+        mix_sb = keep.tile([P, PACK, NPICK], F32, name="mix_sb")
+
+        nc.vector.memset(tab_s[:].bitcast(I32), 0)
+        nc.vector.memset(w2s_raw[:].bitcast(I32), 0)
+
+        def load_scale_rows(queue, plane, scales, row=0, first=0):
+            words = scales.shape[2] // 4
+            for q in range(QUADS):
+                rows = plane[32 * q + row : 32 * q + row + 4, :].bitcast(I32).rearrange("r (a c) -> r a c", a=2)
+                queue.dma_start(
+                    out=rows[:, :, first : first + words],
+                    in_=scales[:, 4 * q : 4 * q + 4, :].bitcast(I32).rearrange("a r c -> r a c"),
+                )
+
+        def load_tab_words(a):
+            nc.sync.dma_start(
+                out=tab_w[a][:].bitcast(I32), in_=tab_words[a].rearrange("p t i -> p (t i)").bitcast(I32)
+            )
+
+        def load_rows(raw, rows):
+            nc.sync.dma_start(out=raw[:], in_=rows.rearrange("(p j) c -> p j c", j=PACK))
+
+        def load_w1(a, b):
+            load_rows(w1_raw[a, b], w1[a * PASS : (a + 1) * PASS, b * PASS : (b + 1) * PASS])
+
+        nc.sync.dma_start(offs_sb[:], offs)
+        load_tab_words(0)
+        load_scale_rows(nc.sync, tab_s, tab_scales)
+        nc.sync.dma_start(
+            out=w2_raw[:].bitcast(I32).rearrange("p (a c) -> p a c", a=2),
+            in_=w2_words.bitcast(I32).rearrange("a p c -> p a c"),
+        )
+        load_w1(0, 0)
+        load_scale_rows(nc.sync, w2s_raw, w2_scales)
+        load_tab_words(1)
+        load_w1(1, 0)
+        nc.gpsimd.dma_start(out=cen_sb[:], in_=cen.rearrange("(b p t) -> p b t", b=2, t=PACK))
+        nc.gpsimd.dma_start(out=gain_sb[:], in_=gain.rearrange("(b p t) -> p b t", b=2, t=PACK))
+        load_scale_rows(nc.sync, w2s_raw, wb_scales, row=4, first=PASS // 4)
+        load_w1(0, 1)
+        load_w1(1, 1)
+        for a in range(2):
+            load_rows(wa_raw[a], wa[a * PASS : (a + 1) * PASS, :])
+        nc.sync.dma_start(
+            out=wb_raw[:].bitcast(I32).rearrange("p (a c) -> p a c", a=2),
+            in_=wb_words.rearrange("a p c i -> a p (c i)").bitcast(I32).rearrange("a p c -> p a c"),
+        )
+        load_rows(mix_sb, mix)
+        nc.sync.dma_start(pos1_sb[:], pos1)
+        nc.sync.dma_start(pos2_sb[:], pos2)
+
+        def dealt(ap):
+            return ap.rearrange("p (g t m) -> p g m t", t=PACK, m=P)
+
+        def undealt(ap):
+            return ap.rearrange("p (g m t) -> p g m t", t=PACK, m=P)
+
+        w2_q = [keep.tile([P, H], U16, name="w2_q%d" % b, align_bytes=64) for b in range(2)]
+        w2_s = [keep.tile([P, H], U8, name="w2_s%d" % b, align_bytes=64) for b in range(2)]
+
+        def block_of(raw, b):
+            return raw[:].rearrange("p (a b m t) -> p a b m t", a=2, b=2, t=PACK)[:, :, b, :, :]
+
+        for b in range(2):
+            nc.scalar.copy(out=dealt(w2_q[b][:]), in_=block_of(w2_raw, b))
+
+        def deal_weight_scales(b):
+            nc.vector.tensor_copy(out=dealt(w2_s[b][:]), in_=block_of(w2s_raw, b))
+
+        nc.sync.dma_start(out=temp_sb[:], in_=temp.rearrange("(p t) -> p t", t=PACK))
+
+        v_q, v_s = {}, {}
+
+        def gather_table(a, half):
+            cols = PASS // LIST_GROUP
+            picks = offs_sb[:, half * cols : (half + 1) * cols]
+            v_q[a, half] = keep.tile([P, PASS], U32, name="v_q%d%d" % (a, half), align_bytes=64)
+            v_s[a, half] = keep.tile([P, PASS], U8, name="v_s%d%d" % (a, half), align_bytes=64)
+            nc.vector.tensor_copy(out=v_q[a, half][:], in_=tab_w[a][:].indirect(picks))
+            nc.vector.tensor_copy(out=v_s[a, half][:], in_=tab_s[:, a * T : (a + 1) * T].indirect(picks))
+
+        def quantise_weight(raw, label, shares):
+            codes = keep.tile([P, PASS], U32, name=label + "_q", align_bytes=64)
+            scales = keep.tile([P, PASS], U8, name=label + "_s", align_bytes=64)
+            for engine, t0, t1 in shares:
+                nt = t1 - t0
+                grouped = ring.tile([P, nt * PASS], BF16, name="w_grouped", tag="w_grouped", bufs=3, align_bytes=64)
+                copy_on(
+                    engine,
+                    grouped[:].rearrange("p (t m j) -> p m j t", t=nt, j=PACK),
+                    raw[:].rearrange("p j (m t) -> p m j t", t=PACK)[:, :, :, t0:t1],
+                )
+                nc.vector.quantize_mx(
+                    out=codes[:, t0 * P : t1 * P].bitcast(FP8X4), scales=scales[:, t0 * P : t1 * P], in_=grouped[:]
+                )
+            return codes, scales
+
+        on_scalar = [("scalar", 0, 4)]
+        on_vector = [("vector", 0, 4)]
+        on_both = [("vector", 0, 2), ("scalar", 2, 4)]
+
+        w1_q = {}
+        gather_table(0, 0)
+        deal_weight_scales(0)
+        w1_q[0, 0] = quantise_weight(w1_raw[0, 0], "w1_00", on_scalar)
+        gather_table(0, 1)
+        gather_table(1, 0)
+        w1_q[1, 0] = quantise_weight(w1_raw[1, 0], "w1_10", on_both)
+        gather_table(1, 1)
+        deal_weight_scales(1)
+
+        def mm_w1(acc, a, b, t, half):
+            codes, scales = w1_q[a, b]
+            cols = slice(t * P, (t + 1) * P)
+            nc.tensor.matmul_mx(
+                out=acc[:], lhsT=codes[:, cols].bitcast(FP8X4), lhsT_scale=scales[:, cols],
+                rhs=v_q[a, half][:].bitcast(FP8X4), rhs_scale=v_s[a, half][:], start=(a == 0), stop=(a == 1),
+            )
+
+        def mm_w2(acc, a, b, t, half):
+            cols = slice(a * PASS + t * P, a * PASS + (t + 1) * P)
+            nc.tensor.matmul_mx(
+                out=acc[:], lhsT=w2_q[b][:, cols].bitcast(FP4X4), lhsT_scale=w2_s[b][:, cols],
+                rhs=v_q[a, half][:].bitcast(FP8X4), rhs_scale=v_s[a, half][:], start=(a == 0), stop=(a == 1),
+            )
+
+        h_q = {}
+
+        def first_stage(b, half, weave_engine, pass_major):
+            lin = [psum.tile([P, PASS], F32, name="lin", tag="acc") for t in range(PACK)] if pass_major else {}
+            proj = [psum.tile([P, PASS], F32, name="proj", tag="acc") for t in range(PACK)] if pass_major else {}
+            if pass_major:
+                for a in range(2):
+                    for t in range(PACK):
+                        mm_w2(lin[t], a, b, t, half)
+                    for t in range(PACK):
+                        mm_w1(proj[t], a, b, t, half)
+            planes = ring.tile([P, PACK, PASS], BF16, name="h_planes", tag="h_planes", align_bytes=64)
+            for t in range(PACK):
+                if not pass_major:
+                    proj[t] = psum.tile([P, PASS], F32, name="proj", tag="acc")
+                    for a in range(2):
+                        mm_w1(proj[t], a, b, t, half)
+                    lin[t] = psum.tile([P, PASS], F32, name="lin", tag="acc")
+                    for a in range(2):
+                        mm_w2(lin[t], a, b, t, half)
+                away = ring.tile([P, PASS], F32, name="away", tag="away", bufs=4)
+                nc.scalar.activation(
+                    out=away[:], in_=proj[t][:], func=ACT.Abs, bias=cen_sb[:, b, t : t + 1], scale=-1.0
+                )
+                nc.vector.scalar_tensor_tensor(
+                    out=planes[:, t, :], in0=away[:], scalar=gain_sb[:, b, t : t + 1], in1=lin[t][:],
+                    op0=ALU.mult, op1=ALU.add,
+                )
+            woven = ring.tile([P, PACK * PASS], BF16, name="h_woven", tag="h_woven", align_bytes=64)
+            copy_on(
+                weave_engine,
+                woven[:].rearrange("p (c i t) -> p c t i", i=4, t=PACK),
+                planes[:].rearrange("p t (c i) -> p c t i", i=4),
+            )
+            codes = keep.tile([P, PASS], U32, name="h_q%d%d" % (b, half), align_bytes=64)
+            scales = keep.tile([P, PASS], U8, name="h_s%d%d" % (b, half), align_bytes=64)
+            nc.vector.quantize_mx(out=codes[:].bitcast(FP8X4), scales=scales[:], in_=woven[:])
+            h_q[b, half] = (codes, scales)
+
+        first_stage(0, 0, "scalar", True)
+        w1_q[0, 1] = quantise_weight(w1_raw[0, 1], "w1_01", on_scalar)
+        w1_q[1, 1] = quantise_weight(w1_raw[1, 1], "w1_11", on_vector)
+        first_stage(0, 1, "vector", False)
+        wa_q = [quantise_weight(wa_raw[0], "wa_0", on_scalar)]
+        first_stage(1, 0, "scalar", False)
+        wa_q.append(quantise_weight(wa_raw[1], "wa_1", on_scalar))
+
+        wb_q = [keep.tile([P, N], U32, name="wb_q%d" % a, align_bytes=64) for a in range(2)]
+        wb_s = [w2_s[1][4:P, a * N : (a + 1) * N] for a in range(2)]
+        neg_temp = keep.tile([P, PACK], F32, name="neg_temp")
+        nc.vector.tensor_scalar(
+            out=neg_temp[:], in0=temp_sb[:], scalar1=-1.0, scalar2=0.0, op0=ALU.mult, op1=ALU.add
+        )
+        for a in range(2):
+            nc.scalar.copy(out=dealt(wb_q[a][:]), in_=undealt(wb_raw[:, a * N : (a + 1) * N]))
+
+        first_stage(1, 1, "vector", False)
+
+        e_sb = [keep.tile([P, S], F32, name="e_sb%d" % t) for t in range(PACK)]
+        d_sb = [keep.tile([P, S], F32, name="d_sb%d" % t) for t in range(PACK)]
+        top = [keep.tile([P, PACK], F32, name="top%d" % half) for half in range(2)]
+        shift = keep.tile([P, PACK], F32, name="shift")
+        y_sb = keep.tile([P, PACK, NPICK], F32, name="y_sb")
+        out_rows = out_0.rearrange("(p t) m -> p t m", t=PACK)
+
+        def second_product(weights, t, half):
+            acc = psum.tile([P, PASS], F32, name="acc2", tag="acc")
+            cols = slice(t * P, (t + 1) * P)
+            for b in range(2):
+                codes, scales = weights[b]
+                nc.tensor.matmul_mx(
+                    out=acc[:], lhsT=codes[:, cols].bitcast(FP8X4), lhsT_scale=scales[:, cols],
+                    rhs=h_q[b, half][0][:].bitcast(FP8X4), rhs_scale=h_q[b, half][1][:],
+                    start=(b == 0), stop=(b == 1),
+                )
+            return acc
+
+        wb_pair = list(zip(wb_q, wb_s))
+        for half in range(2):
+            cols = slice(half * PASS, (half + 1) * PASS)
+            for t in range(PACK):
+                acc_e = second_product(wa_q, t, half)
+                nc.vector.tensor_scalar(
+                    out=e_sb[t][:, cols], in0=acc_e[:], scalar1=1.0,
+                    scalar2=(None if half == 0 else top[0][:, t : t + 1]),
+                    op0=ALU.mult, op1=ALU.max, accum_out=top[half][:, t : t + 1],
+                )
+                acc_d = second_product(wb_pair, t, half)
+                nc.scalar.copy(out=d_sb[t][:, cols], in_=acc_d[:])
+
+        for t in range(PACK):
+            nc.scalar.activation(
+                out=shift[:, t : t + 1], in_=top[1][:, t : t + 1], func=ACT.Copy, scale=neg_temp[:, t : t + 1]
+            )
+            weight = ring.tile([P, NPICK], F32, name="weight", tag="weight", bufs=4)
+            nc.scalar.activation(
+                out=weight[:], in_=e_sb[t][:].indirect(pos1_sb[:]), func=ACT.Exp,
+                bias=shift[:, t : t + 1], scale=temp_sb[:, t : t + 1],
+            )
+            mixed = ring.tile([P, NPICK], F32, name="mixed", tag="mixed", bufs=4)
+            nc.vector.tensor_tensor(
+                out=mixed[:], in0=d_sb[t][:].indirect(pos2_sb[:]), in1=mix_sb[:, t, :], op=ALU.mult
+            )
+            nc.vector.tensor_tensor(out=y_sb[:, t, :], in0=weight[:], in1=mixed[:], op=ALU.mult)
+            nc.sync.dma_start(out=out_rows[:, t, :], in_=y_sb[:, t, :])
+
+        y_q = keep.tile([P, NPICK], U32, name="y_q", align_bytes=64)
+        y_s = keep.tile([P, NPICK], U8, name="y_s", align_bytes=64)
+        width = NPICK // 2
+        for part, engine in enumerate(("vector", "scalar")):
+            cols = slice(part * width, (part + 1) * width)
+            y_woven = ring.tile([P, PACK * width], BF16, name="y_woven", tag="y_woven", align_bytes=64)
+            copy_on(
+                engine,
+                y_woven[:].rearrange("p (c i t) -> p c t i", i=4, t=PACK),
+                y_sb[:, :, cols].rearrange("p t (c i) -> p c t i", i=4),
+            )
+            nc.vector.quantize_mx(out=y_q[:, cols].bitcast(FP8X4), scales=y_s[:, cols], in_=y_woven[:])
+        nc.sync.dma_start(
+            out=out_1[0].rearrange("p m i -> p (m i)").bitcast(I32), in_=y_q[:].bitcast(I32)
+        )
+        for q in range(QUADS):
+            queue = nc.sync if q % 2 == 0 else nc.scalar
+            queue.dma_start(
+                out=out_2[0, 4 * q : 4 * q + 4, :].bitcast(I32), in_=y_s[32 * q : 32 * q + 4, :].bitcast(I32)
+            )

@@ -38,25 +38,31 @@ def tile_list_streak_linkage_features_kernel(
     with ExitStack() as ctx:
         keep = ctx.enter_context(tc.tile_pool(name="keep", bufs=1))
         ring = ctx.enter_context(tc.tile_pool(name="ring", bufs=2))
+        staged = ctx.enter_context(tc.tile_pool(name="staged", bufs=3))
         psum = ctx.enter_context(tc.psum_pool(name="psum", bufs=8))
 
         offs_sb = keep.tile([P, S // LIST_GROUP], U16, name="offs_sb")
         pos1_sb = keep.tile([P, NPICK // LIST_GROUP], U16, name="pos1_sb")
         pos2_sb = keep.tile([P, NPICK // LIST_GROUP], U16, name="pos2_sb")
         tab_w = [keep.tile([P, T], U32, name="tab_w%d" % a, align_bytes=64) for a in range(2)]
-        tab_s = keep.tile([P, 2 * T], U8, name="tab_s", align_bytes=64)
-        w2_raw = keep.tile([P, 2 * H], U16, name="w2_raw", align_bytes=64)
+        tab_s = keep.tile([P, T], U8, name="tab_s", align_bytes=64)
+        w2_raw = staged.tile([P, 2 * H], U16, name="w2_raw", tag="raw")
         w2s_raw = keep.tile([P, 2 * H], U8, name="w2s_raw", align_bytes=64)
-        wb_raw = keep.tile([P, 2 * N], U32, name="wb_raw", align_bytes=64)
-        w1_raw = {(a, b): keep.tile([P, PACK, PASS], F32, name="w1_raw%d%d" % (a, b)) for a in range(2) for b in range(2)}
-        wa_raw = [keep.tile([P, PACK, N], F32, name="wa_raw%d" % a) for a in range(2)]
+        w1_raw = {(a, 0): staged.tile([P, PACK, PASS], F32, name="w1_raw%d0" % a, tag="raw") for a in range(2)}
+        for a in range(2):
+            w1_raw[a, 1] = staged.tile([P, PACK, PASS], F32, name="w1_raw%d1" % a, tag="raw")
+        wa_raw = [staged.tile([P, PACK, N], F32, name="wa_raw%d" % a, tag="raw") for a in range(2)]
+        wb_raw = staged.tile([P, 2 * N], U32, name="wb_raw", tag="raw")
         cen_sb = keep.tile([P, 2, PACK], F32, name="cen_sb")
         gain_sb = keep.tile([P, 2, PACK], F32, name="gain_sb")
         temp_sb = keep.tile([P, PACK], F32, name="temp_sb")
-        mix_sb = keep.tile([P, PACK, NPICK], F32, name="mix_sb")
+        mix_sb = staged.tile([P, PACK, NPICK], F32, name="mix_sb", tag="raw")
 
-        nc.vector.memset(tab_s[:].bitcast(I32), 0)
+        nc.gpsimd.memset(tab_s[:].bitcast(I32), 0)
         nc.vector.memset(w2s_raw[:].bitcast(I32), 0)
+        v_s_low = keep.tile([P, S], U8, name="v_s_low", align_bytes=64)
+        nc.vector.memset(v_s_low[:].bitcast(I32), 0)
+
 
         def load_scale_rows(queue, plane, scales, row=0, first=0):
             words = scales.shape[2] // 4
@@ -79,30 +85,36 @@ def tile_list_streak_linkage_features_kernel(
             load_rows(w1_raw[a, b], w1[a * PASS : (a + 1) * PASS, b * PASS : (b + 1) * PASS])
 
         nc.sync.dma_start(offs_sb[:], offs)
-        load_tab_words(0)
-        load_scale_rows(nc.sync, tab_s, tab_scales)
         nc.sync.dma_start(
             out=w2_raw[:].bitcast(I32).rearrange("p (a c) -> p a c", a=2),
             in_=w2_words.bitcast(I32).rearrange("a p c -> p a c"),
         )
+        for q in range(QUADS):
+            nc.sync.dma_start(
+                out=tab_s[32 * q : 32 * q + 8, :].bitcast(I32), in_=tab_scales[:, 4 * q : 4 * q + 4, :].bitcast(I32)
+            )
+        load_tab_words(0)
         load_w1(0, 0)
         load_scale_rows(nc.sync, w2s_raw, w2_scales)
-        load_tab_words(1)
         load_w1(1, 0)
+        load_scale_rows(nc.sync, w2s_raw, wb_scales, row=4, first=PASS // 4)
+        load_tab_words(1)
         nc.gpsimd.dma_start(out=cen_sb[:], in_=cen.rearrange("(b p t) -> p b t", b=2, t=PACK))
         nc.gpsimd.dma_start(out=gain_sb[:], in_=gain.rearrange("(b p t) -> p b t", b=2, t=PACK))
-        load_scale_rows(nc.sync, w2s_raw, wb_scales, row=4, first=PASS // 4)
-        load_w1(0, 1)
-        load_w1(1, 1)
-        for a in range(2):
-            load_rows(wa_raw[a], wa[a * PASS : (a + 1) * PASS, :])
-        nc.sync.dma_start(
-            out=wb_raw[:].bitcast(I32).rearrange("p (a c) -> p a c", a=2),
-            in_=wb_words.rearrange("a p c i -> a p (c i)").bitcast(I32).rearrange("a p c -> p a c"),
-        )
-        load_rows(mix_sb, mix)
-        nc.sync.dma_start(pos1_sb[:], pos1)
-        nc.sync.dma_start(pos2_sb[:], pos2)
+        nc.gpsimd.dma_start(out=temp_sb[:], in_=temp.rearrange("(p t) -> p t", t=PACK))
+
+        def load_later():
+            load_w1(0, 1)
+            load_w1(1, 1)
+            for a in range(2):
+                load_rows(wa_raw[a], wa[a * PASS : (a + 1) * PASS, :])
+            nc.sync.dma_start(
+                out=wb_raw[:].bitcast(I32).rearrange("p (a c) -> p a c", a=2),
+                in_=wb_words.rearrange("a p c i -> a p (c i)").bitcast(I32).rearrange("a p c -> p a c"),
+            )
+            load_rows(mix_sb, mix)
+            nc.sync.dma_start(pos1_sb[:], pos1)
+            nc.sync.dma_start(pos2_sb[:], pos2)
 
         def dealt(ap):
             return ap.rearrange("p (g t m) -> p g m t", t=PACK, m=P)
@@ -122,24 +134,30 @@ def tile_list_streak_linkage_features_kernel(
         def deal_weight_scales(b):
             nc.vector.tensor_copy(out=dealt(w2_s[b][:]), in_=block_of(w2s_raw, b))
 
-        nc.sync.dma_start(out=temp_sb[:], in_=temp.rearrange("(p t) -> p t", t=PACK))
+        v_q = {}
+        v_s = keep.tile([P, S], U8, name="v_s", align_bytes=64)
 
-        v_q, v_s = {}, {}
+        def picks_of(half):
+            cols = PASS // LIST_GROUP
+            return offs_sb[:, half * cols : (half + 1) * cols]
+
+        def gather_scales(half):
+            nc.vector.tensor_copy(out=v_s[:, half * PASS : (half + 1) * PASS], in_=tab_s[:].indirect(picks_of(half)))
 
         def gather_table(a, half):
-            cols = PASS // LIST_GROUP
-            picks = offs_sb[:, half * cols : (half + 1) * cols]
-            v_q[a, half] = keep.tile([P, PASS], U32, name="v_q%d%d" % (a, half), align_bytes=64)
-            v_s[a, half] = keep.tile([P, PASS], U8, name="v_s%d%d" % (a, half), align_bytes=64)
-            nc.vector.tensor_copy(out=v_q[a, half][:], in_=tab_w[a][:].indirect(picks))
-            nc.vector.tensor_copy(out=v_s[a, half][:], in_=tab_s[:, a * T : (a + 1) * T].indirect(picks))
+            tag = "v_q%d%d" % (a, half)
+            v_q[a, half] = keep.tile([P, PASS], U32, name="v_q%d%d" % (a, half), tag=tag, align_bytes=64)
+            nc.vector.tensor_copy(out=v_q[a, half][:], in_=tab_w[a][:].indirect(picks_of(half)))
 
         def quantise_weight(raw, label, shares):
             codes = keep.tile([P, PASS], U32, name=label + "_q", align_bytes=64)
             scales = keep.tile([P, PASS], U8, name=label + "_s", align_bytes=64)
             for engine, t0, t1 in shares:
                 nt = t1 - t0
-                grouped = ring.tile([P, nt * PASS], BF16, name="w_grouped", tag="w_grouped", bufs=3, align_bytes=64)
+                if engine == "vector" and nt == 2:
+                    grouped = keep.tile([P, nt * PASS], BF16, name="w_first", tag="w_first", align_bytes=64)
+                else:
+                    grouped = ring.tile([P, nt * PASS], BF16, name="w_grouped", tag="w_grouped", bufs=3, align_bytes=64)
                 copy_on(
                     engine,
                     grouped[:].rearrange("p (t m j) -> p m j t", t=nt, j=PACK),
@@ -155,42 +173,55 @@ def tile_list_streak_linkage_features_kernel(
         on_both = [("vector", 0, 2), ("scalar", 2, 4)]
 
         w1_q = {}
+        gather_scales(0)
+        gather_scales(1)
         gather_table(0, 0)
+        for q in range(QUADS):
+            nc.sync.dma_start(
+                out=v_s_low[32 * q : 32 * q + 4, :].bitcast(I32), in_=v_s[32 * q + 4 : 32 * q + 8, :].bitcast(I32)
+            )
+        load_later()
         deal_weight_scales(0)
         w1_q[0, 0] = quantise_weight(w1_raw[0, 0], "w1_00", on_scalar)
         gather_table(0, 1)
-        gather_table(1, 0)
-        w1_q[1, 0] = quantise_weight(w1_raw[1, 0], "w1_10", on_both)
-        gather_table(1, 1)
         deal_weight_scales(1)
+        w1_q[1, 0] = quantise_weight(w1_raw[1, 0], "w1_10", on_scalar)
+        gather_table(1, 0)
+        gather_table(1, 1)
 
         def mm_w1(acc, a, b, t, half):
             codes, scales = w1_q[a, b]
             cols = slice(t * P, (t + 1) * P)
             nc.tensor.matmul_mx(
                 out=acc[:], lhsT=codes[:, cols].bitcast(FP8X4), lhsT_scale=scales[:, cols],
-                rhs=v_q[a, half][:].bitcast(FP8X4), rhs_scale=v_s[a, half][:], start=(a == 0), stop=(a == 1),
+                rhs=v_q[a, half][:].bitcast(FP8X4), rhs_scale=v_s[4 * a : P, half * PASS : (half + 1) * PASS], start=(a == 0), stop=(a == 1),
             )
 
         def mm_w2(acc, a, b, t, half):
             cols = slice(a * PASS + t * P, a * PASS + (t + 1) * P)
             nc.tensor.matmul_mx(
                 out=acc[:], lhsT=w2_q[b][:, cols].bitcast(FP4X4), lhsT_scale=w2_s[b][:, cols],
-                rhs=v_q[a, half][:].bitcast(FP8X4), rhs_scale=v_s[a, half][:], start=(a == 0), stop=(a == 1),
+                rhs=v_q[a, half][:].bitcast(FP8X4),
+                rhs_scale=(v_s, v_s_low)[a][:, half * PASS : (half + 1) * PASS], start=(a == 0), stop=(a == 1),
             )
 
         h_q = {}
 
-        def first_stage(b, half, weave_engine, pass_major):
+        h_planes = {}
+
+        def first_stage(b, half, pass_major):
             lin = [psum.tile([P, PASS], F32, name="lin", tag="acc") for t in range(PACK)] if pass_major else {}
             proj = [psum.tile([P, PASS], F32, name="proj", tag="acc") for t in range(PACK)] if pass_major else {}
             if pass_major:
-                for a in range(2):
-                    for t in range(PACK):
-                        mm_w2(lin[t], a, b, t, half)
-                    for t in range(PACK):
-                        mm_w1(proj[t], a, b, t, half)
-            planes = ring.tile([P, PACK, PASS], BF16, name="h_planes", tag="h_planes", align_bytes=64)
+                for t in range(PACK):
+                    mm_w2(lin[t], 0, b, t, half)
+                for t in range(PACK):
+                    mm_w1(proj[t], 0, b, t, half)
+                for t in range(PACK):
+                    mm_w1(proj[t], 1, b, t, half)
+                    mm_w2(lin[t], 1, b, t, half)
+            planes = keep.tile([P, PACK, PASS], BF16, name="h_planes%d%d" % (b, half), align_bytes=64)
+            h_planes[b, half] = planes
             for t in range(PACK):
                 if not pass_major:
                     proj[t] = psum.tile([P, PASS], F32, name="proj", tag="acc")
@@ -207,6 +238,9 @@ def tile_list_streak_linkage_features_kernel(
                     out=planes[:, t, :], in0=away[:], scalar=gain_sb[:, b, t : t + 1], in1=lin[t][:],
                     op0=ALU.mult, op1=ALU.add,
                 )
+
+        def quantise_h(b, half, weave_engine):
+            planes = h_planes[b, half]
             woven = ring.tile([P, PACK * PASS], BF16, name="h_woven", tag="h_woven", align_bytes=64)
             copy_on(
                 weave_engine,
@@ -218,24 +252,26 @@ def tile_list_streak_linkage_features_kernel(
             nc.vector.quantize_mx(out=codes[:].bitcast(FP8X4), scales=scales[:], in_=woven[:])
             h_q[b, half] = (codes, scales)
 
-        first_stage(0, 0, "scalar", True)
-        w1_q[0, 1] = quantise_weight(w1_raw[0, 1], "w1_01", on_scalar)
-        w1_q[1, 1] = quantise_weight(w1_raw[1, 1], "w1_11", on_vector)
-        first_stage(0, 1, "vector", False)
-        wa_q = [quantise_weight(wa_raw[0], "wa_0", on_scalar)]
-        first_stage(1, 0, "scalar", False)
-        wa_q.append(quantise_weight(wa_raw[1], "wa_1", on_scalar))
-
-        wb_q = [keep.tile([P, N], U32, name="wb_q%d" % a, align_bytes=64) for a in range(2)]
         wb_s = [w2_s[1][4:P, a * N : (a + 1) * N] for a in range(2)]
         neg_temp = keep.tile([P, PACK], F32, name="neg_temp")
+        wa_q = {}
+        first_stage(0, 0, True)
+        w1_q[0, 1] = quantise_weight(w1_raw[0, 1], "w1_01", on_vector)
+        w1_q[1, 1] = quantise_weight(w1_raw[1, 1], "w1_11", on_scalar)
+        first_stage(0, 1, False)
+        quantise_h(0, 0, "vector")
+        first_stage(1, 0, False)
+        wa_q[0] = quantise_weight(wa_raw[0], "wa_0", on_scalar)
+        quantise_h(1, 0, "vector")
+        wa_q[1] = quantise_weight(wa_raw[1], "wa_1", on_scalar)
+        wb_q = keep.tile([P, 2 * N], U32, name="wb_q", align_bytes=64)
+        nc.scalar.copy(out=dealt(wb_q[:]), in_=undealt(wb_raw[:]))
         nc.vector.tensor_scalar(
             out=neg_temp[:], in0=temp_sb[:], scalar1=-1.0, scalar2=0.0, op0=ALU.mult, op1=ALU.add
         )
-        for a in range(2):
-            nc.scalar.copy(out=dealt(wb_q[a][:]), in_=undealt(wb_raw[:, a * N : (a + 1) * N]))
-
-        first_stage(1, 1, "vector", False)
+        first_stage(1, 1, False)
+        quantise_h(0, 1, "scalar")
+        quantise_h(1, 1, "vector")
 
         e_sb = [keep.tile([P, S], F32, name="e_sb%d" % t) for t in range(PACK)]
         d_sb = [keep.tile([P, S], F32, name="d_sb%d" % t) for t in range(PACK)]
@@ -256,7 +292,7 @@ def tile_list_streak_linkage_features_kernel(
                 )
             return acc
 
-        wb_pair = list(zip(wb_q, wb_s))
+        wb_pair = [(wb_q[:, a * N : (a + 1) * N], wb_s[a]) for a in range(2)]
         for half in range(2):
             cols = slice(half * PASS, (half + 1) * PASS)
             for t in range(PACK):

@@ -60,9 +60,10 @@ def tile_list_streak_linkage_features_kernel(
 
         nc.gpsimd.memset(tab_s[:].bitcast(I32), 0)
         nc.vector.memset(w2s_raw[:].bitcast(I32), 0)
-        v_s_low = keep.tile([P, S], U8, name="v_s_low", align_bytes=64)
-        nc.vector.memset(v_s_low[:].bitcast(I32), 0)
-
+        v_s = [keep.tile([P, S], U8, name="v_s%d" % a, align_bytes=64) for a in range(2)]
+        for a in range(2):
+            nc.vector.memset(v_s[a][:].bitcast(I32), 0)
+        picked_s = keep.tile([P, S], U8, name="picked_s", align_bytes=64)
 
         def load_scale_rows(queue, plane, scales, row=0, first=0):
             words = scales.shape[2] // 4
@@ -84,24 +85,32 @@ def tile_list_streak_linkage_features_kernel(
         def load_w1(a, b):
             load_rows(w1_raw[a, b], w1[a * PASS : (a + 1) * PASS, b * PASS : (b + 1) * PASS])
 
+        def move_scale_rows(a):
+            for q in range(QUADS):
+                first = 64 * a + 16 * q
+                nc.sync.dma_start(
+                    out=v_s[a][32 * q : 32 * q + 4, :].bitcast(I32), in_=picked_s[first : first + 16 : 4, :].bitcast(I32)
+                )
+
         nc.sync.dma_start(offs_sb[:], offs)
         nc.sync.dma_start(
             out=w2_raw[:].bitcast(I32).rearrange("p (a c) -> p a c", a=2),
             in_=w2_words.bitcast(I32).rearrange("a p c -> p a c"),
         )
-        for q in range(QUADS):
-            nc.sync.dma_start(
-                out=tab_s[32 * q : 32 * q + 8, :].bitcast(I32), in_=tab_scales[:, 4 * q : 4 * q + 4, :].bitcast(I32)
-            )
+        nc.sync.dma_start(
+            out=tab_s[0:P:4, :].bitcast(I32), in_=tab_scales.rearrange("a q c -> (a q) c").bitcast(I32)
+        )
+        nc.vector.tensor_copy(out=picked_s[:], in_=tab_s[:].indirect(offs_sb[:]))
         load_tab_words(0)
-        load_w1(0, 0)
         load_scale_rows(nc.sync, w2s_raw, w2_scales)
-        load_w1(1, 0)
+        load_w1(0, 0)
         load_scale_rows(nc.sync, w2s_raw, wb_scales, row=4, first=PASS // 4)
         load_tab_words(1)
+        move_scale_rows(0)
+        load_w1(1, 0)
+        move_scale_rows(1)
         nc.gpsimd.dma_start(out=cen_sb[:], in_=cen.rearrange("(b p t) -> p b t", b=2, t=PACK))
         nc.gpsimd.dma_start(out=gain_sb[:], in_=gain.rearrange("(b p t) -> p b t", b=2, t=PACK))
-        nc.gpsimd.dma_start(out=temp_sb[:], in_=temp.rearrange("(p t) -> p t", t=PACK))
 
         def load_later():
             load_w1(0, 1)
@@ -115,6 +124,7 @@ def tile_list_streak_linkage_features_kernel(
             load_rows(mix_sb, mix)
             nc.sync.dma_start(pos1_sb[:], pos1)
             nc.sync.dma_start(pos2_sb[:], pos2)
+            nc.sync.dma_start(out=temp_sb[:], in_=temp.rearrange("(p t) -> p t", t=PACK))
 
         def dealt(ap):
             return ap.rearrange("p (g t m) -> p g m t", t=PACK, m=P)
@@ -126,23 +136,22 @@ def tile_list_streak_linkage_features_kernel(
         w2_s = [keep.tile([P, H], U8, name="w2_s%d" % b, align_bytes=64) for b in range(2)]
 
         def block_of(raw, b):
-            return raw[:].rearrange("p (a b m t) -> p a b m t", a=2, b=2, t=PACK)[:, :, b, :, :]
+            return raw[:].rearrange("p (a b m t) -> p a b t m", a=2, b=2, t=PACK)[:, :, b, :, :]
 
-        for b in range(2):
-            nc.scalar.copy(out=dealt(w2_q[b][:]), in_=block_of(w2_raw, b))
+        def in_order(dealt_tile):
+            return dealt_tile[:].rearrange("p (a t m) -> p a t m", a=2, t=PACK)
+
+        def deal_w2_words(b):
+            nc.scalar.copy(out=in_order(w2_q[b]), in_=block_of(w2_raw, b))
 
         def deal_weight_scales(b):
-            nc.vector.tensor_copy(out=dealt(w2_s[b][:]), in_=block_of(w2s_raw, b))
+            nc.vector.tensor_copy(out=in_order(w2_s[b]), in_=block_of(w2s_raw, b))
 
         v_q = {}
-        v_s = keep.tile([P, S], U8, name="v_s", align_bytes=64)
 
         def picks_of(half):
             cols = PASS // LIST_GROUP
             return offs_sb[:, half * cols : (half + 1) * cols]
-
-        def gather_scales(half):
-            nc.vector.tensor_copy(out=v_s[:, half * PASS : (half + 1) * PASS], in_=tab_s[:].indirect(picks_of(half)))
 
         def gather_table(a, half):
             tag = "v_q%d%d" % (a, half)
@@ -173,28 +182,24 @@ def tile_list_streak_linkage_features_kernel(
         on_both = [("vector", 0, 2), ("scalar", 2, 4)]
 
         w1_q = {}
-        gather_scales(0)
-        gather_scales(1)
         gather_table(0, 0)
-        for q in range(QUADS):
-            nc.sync.dma_start(
-                out=v_s_low[32 * q : 32 * q + 4, :].bitcast(I32), in_=v_s[32 * q + 4 : 32 * q + 8, :].bitcast(I32)
-            )
+        gather_table(0, 1)
         load_later()
+        deal_w2_words(0)
+        deal_w2_words(1)
         deal_weight_scales(0)
         w1_q[0, 0] = quantise_weight(w1_raw[0, 0], "w1_00", on_scalar)
-        gather_table(0, 1)
         deal_weight_scales(1)
-        w1_q[1, 0] = quantise_weight(w1_raw[1, 0], "w1_10", on_scalar)
         gather_table(1, 0)
         gather_table(1, 1)
+        w1_q[1, 0] = quantise_weight(w1_raw[1, 0], "w1_10", on_both)
 
         def mm_w1(acc, a, b, t, half):
             codes, scales = w1_q[a, b]
             cols = slice(t * P, (t + 1) * P)
             nc.tensor.matmul_mx(
                 out=acc[:], lhsT=codes[:, cols].bitcast(FP8X4), lhsT_scale=scales[:, cols],
-                rhs=v_q[a, half][:].bitcast(FP8X4), rhs_scale=v_s[4 * a : P, half * PASS : (half + 1) * PASS], start=(a == 0), stop=(a == 1),
+                rhs=v_q[a, half][:].bitcast(FP8X4), rhs_scale=v_s[a][:, half * PASS : (half + 1) * PASS], start=(a == 0), stop=(a == 1),
             )
 
         def mm_w2(acc, a, b, t, half):
@@ -202,7 +207,7 @@ def tile_list_streak_linkage_features_kernel(
             nc.tensor.matmul_mx(
                 out=acc[:], lhsT=w2_q[b][:, cols].bitcast(FP4X4), lhsT_scale=w2_s[b][:, cols],
                 rhs=v_q[a, half][:].bitcast(FP8X4),
-                rhs_scale=(v_s, v_s_low)[a][:, half * PASS : (half + 1) * PASS], start=(a == 0), stop=(a == 1),
+                rhs_scale=v_s[a][:, half * PASS : (half + 1) * PASS], start=(a == 0), stop=(a == 1),
             )
 
         h_q = {}

@@ -20,7 +20,11 @@ P = 128
 PACK = 4
 PASS = P * PACK
 QUADS = 4
+QUAD = P // QUADS
+LIVE = 4
 LIST_GROUP = 16
+SPREAD = 4
+RUN = 4
 
 
 def tile_list_streak_linkage_features_kernel(
@@ -47,11 +51,12 @@ def tile_list_streak_linkage_features_kernel(
         tab_w = [keep.tile([P, T], U32, name="tab_w%d" % a, align_bytes=64) for a in range(2)]
         tab_s = keep.tile([P, T], U8, name="tab_s", align_bytes=64)
         w2_raw = staged.tile([P, 2 * H], U16, name="w2_raw", tag="raw")
-        w2s_raw = keep.tile([P, 2 * H], U8, name="w2s_raw", align_bytes=64)
-        w1_raw = {(a, 0): staged.tile([P, PACK, PASS], F32, name="w1_raw%d0" % a, tag="raw") for a in range(2)}
-        for a in range(2):
-            w1_raw[a, 1] = staged.tile([P, PACK, PASS], F32, name="w1_raw%d1" % a, tag="raw")
-        wa_raw = [staged.tile([P, PACK, N], F32, name="wa_raw%d" % a, tag="raw") for a in range(2)]
+        weight_s_raw = keep.tile([P, 2 * H], U8, name="weight_s_raw", align_bytes=64)
+        w1_raw = {
+            (a, b): staged.tile([P, PACK, PASS], F32, name="w1_raw%d%d" % (a, b), tag="raw")
+            for b in range(2) for a in range(2)
+        }
+        wa_raw = [staged.tile([P, PACK, N], F32, name="wa_raw%d" % b, tag="raw") for b in range(2)]
         wb_raw = staged.tile([P, 2 * N], U32, name="wb_raw", tag="raw")
         cen_sb = keep.tile([P, 2, PACK], F32, name="cen_sb")
         gain_sb = keep.tile([P, 2, PACK], F32, name="gain_sb")
@@ -59,24 +64,24 @@ def tile_list_streak_linkage_features_kernel(
         mix_sb = staged.tile([P, PACK, NPICK], F32, name="mix_sb", tag="raw")
 
         nc.gpsimd.memset(tab_s[:].bitcast(I32), 0)
-        nc.vector.memset(w2s_raw[:].bitcast(I32), 0)
+        nc.vector.memset(weight_s_raw[:].bitcast(I32), 0)
         v_s = [keep.tile([P, S], U8, name="v_s%d" % a, align_bytes=64) for a in range(2)]
         for a in range(2):
             nc.vector.memset(v_s[a][:].bitcast(I32), 0)
         picked_s = keep.tile([P, S], U8, name="picked_s", align_bytes=64)
 
-        def load_scale_rows(queue, plane, scales, row=0, first=0):
-            words = scales.shape[2] // 4
+        def load_weight_scales(scales, row, first_byte):
+            width = scales.shape[2]
             for q in range(QUADS):
-                rows = plane[32 * q + row : 32 * q + row + 4, :].bitcast(I32).rearrange("r (a c) -> r a c", a=2)
-                queue.dma_start(
-                    out=rows[:, :, first : first + words],
-                    in_=scales[:, 4 * q : 4 * q + 4, :].bitcast(I32).rearrange("a r c -> r a c"),
+                rows = weight_s_raw[QUAD * q + row : QUAD * q + row + LIVE, :].bitcast(I32)
+                nc.sync.dma_start(
+                    out=rows.rearrange("r (g c) -> r g c", g=2)[:, :, first_byte // 4 : (first_byte + width) // 4],
+                    in_=scales[:, LIVE * q : LIVE * (q + 1), :].bitcast(I32).rearrange("g r c -> r g c"),
                 )
 
         def load_tab_words(a):
             nc.sync.dma_start(
-                out=tab_w[a][:].bitcast(I32), in_=tab_words[a].rearrange("p t i -> p (t i)").bitcast(I32)
+                out=tab_w[a][:].bitcast(I32), in_=tab_words[a].rearrange("p c i -> p (c i)").bitcast(I32)
             )
 
         def load_rows(raw, rows):
@@ -85,11 +90,12 @@ def tile_list_streak_linkage_features_kernel(
         def load_w1(a, b):
             load_rows(w1_raw[a, b], w1[a * PASS : (a + 1) * PASS, b * PASS : (b + 1) * PASS])
 
-        def move_scale_rows(a):
+        def move_table_scales(a):
             for q in range(QUADS):
-                first = 64 * a + 16 * q
+                first = SPREAD * LIVE * (QUADS * a + q)
                 nc.sync.dma_start(
-                    out=v_s[a][32 * q : 32 * q + 4, :].bitcast(I32), in_=picked_s[first : first + 16 : 4, :].bitcast(I32)
+                    out=v_s[a][QUAD * q : QUAD * q + LIVE, :].bitcast(I32),
+                    in_=picked_s[first : first + SPREAD * LIVE : SPREAD, :].bitcast(I32),
                 )
 
         nc.sync.dma_start(offs_sb[:], offs)
@@ -98,183 +104,193 @@ def tile_list_streak_linkage_features_kernel(
             in_=w2_words.bitcast(I32).rearrange("a p c -> p a c"),
         )
         nc.sync.dma_start(
-            out=tab_s[0:P:4, :].bitcast(I32), in_=tab_scales.rearrange("a q c -> (a q) c").bitcast(I32)
+            out=tab_s[0:P:SPREAD, :].bitcast(I32), in_=tab_scales.rearrange("a i c -> (a i) c").bitcast(I32)
         )
         nc.vector.tensor_copy(out=picked_s[:], in_=tab_s[:].indirect(offs_sb[:]))
         load_tab_words(0)
-        load_scale_rows(nc.sync, w2s_raw, w2_scales)
+        load_weight_scales(w2_scales, 0, 0)
         load_w1(0, 0)
-        load_scale_rows(nc.sync, w2s_raw, wb_scales, row=4, first=PASS // 4)
+        load_weight_scales(wb_scales, LIVE, PASS)
         load_tab_words(1)
-        move_scale_rows(0)
+        move_table_scales(0)
         load_w1(1, 0)
-        move_scale_rows(1)
+        move_table_scales(1)
         nc.gpsimd.dma_start(out=cen_sb[:], in_=cen.rearrange("(b p t) -> p b t", b=2, t=PACK))
         nc.gpsimd.dma_start(out=gain_sb[:], in_=gain.rearrange("(b p t) -> p b t", b=2, t=PACK))
 
-        def load_later():
+        def load_later_operands():
             load_w1(0, 1)
             load_w1(1, 1)
-            for a in range(2):
-                load_rows(wa_raw[a], wa[a * PASS : (a + 1) * PASS, :])
+            for b in range(2):
+                load_rows(wa_raw[b], wa[b * PASS : (b + 1) * PASS, :])
             nc.sync.dma_start(
-                out=wb_raw[:].bitcast(I32).rearrange("p (a c) -> p a c", a=2),
-                in_=wb_words.rearrange("a p c i -> a p (c i)").bitcast(I32).rearrange("a p c -> p a c"),
+                out=wb_raw[:].bitcast(I32).rearrange("p (b c) -> p b c", b=2),
+                in_=wb_words.rearrange("b p c i -> b p (c i)").bitcast(I32).rearrange("b p c -> p b c"),
             )
             load_rows(mix_sb, mix)
             nc.sync.dma_start(pos1_sb[:], pos1)
             nc.sync.dma_start(pos2_sb[:], pos2)
             nc.sync.dma_start(out=temp_sb[:], in_=temp.rearrange("(p t) -> p t", t=PACK))
 
-        def dealt(ap):
-            return ap.rearrange("p (g t m) -> p g m t", t=PACK, m=P)
-
-        def undealt(ap):
-            return ap.rearrange("p (g m t) -> p g m t", t=PACK, m=P)
-
         w2_q = [keep.tile([P, H], U16, name="w2_q%d" % b, align_bytes=64) for b in range(2)]
-        w2_s = [keep.tile([P, H], U8, name="w2_s%d" % b, align_bytes=64) for b in range(2)]
+        weight_s = [keep.tile([P, H], U8, name="weight_s%d" % b, align_bytes=64) for b in range(2)]
 
         def block_of(raw, b):
             return raw[:].rearrange("p (a b m t) -> p a b t m", a=2, b=2, t=PACK)[:, :, b, :, :]
 
-        def in_order(dealt_tile):
-            return dealt_tile[:].rearrange("p (a t m) -> p a t m", a=2, t=PACK)
+        def places_of(dealt):
+            return dealt[:].rearrange("p (a t m) -> p a t m", a=2, t=PACK)
 
         def deal_w2_words(b):
-            nc.scalar.copy(out=in_order(w2_q[b]), in_=block_of(w2_raw, b))
+            nc.scalar.copy(out=places_of(w2_q[b]), in_=block_of(w2_raw, b))
 
         def deal_weight_scales(b):
-            nc.vector.tensor_copy(out=in_order(w2_s[b]), in_=block_of(w2s_raw, b))
+            nc.vector.tensor_copy(out=places_of(weight_s[b]), in_=block_of(weight_s_raw, b))
 
         v_q = {}
 
-        def picks_of(half):
-            cols = PASS // LIST_GROUP
-            return offs_sb[:, half * cols : (half + 1) * cols]
-
         def gather_table(a, half):
-            tag = "v_q%d%d" % (a, half)
-            v_q[a, half] = keep.tile([P, PASS], U32, name="v_q%d%d" % (a, half), tag=tag, align_bytes=64)
-            nc.vector.tensor_copy(out=v_q[a, half][:], in_=tab_w[a][:].indirect(picks_of(half)))
+            cols = PASS // LIST_GROUP
+            v_q[a, half] = keep.tile([P, PASS], U32, name="v_q%d%d" % (a, half), align_bytes=64)
+            nc.vector.tensor_copy(
+                out=v_q[a, half][:], in_=tab_w[a][:].indirect(offs_sb[:, half * cols : (half + 1) * cols])
+            )
 
-        def quantise_weight(raw, label, shares):
+        def round_pair(engine, grouped, raw, pair):
+            copy_on(
+                engine,
+                grouped[:, 2 * pair * PASS : 2 * (pair + 1) * PASS].rearrange("p (t m j) -> p m j t", t=2, j=PACK),
+                raw[:].rearrange("p j (m t) -> p m j t", t=PACK)[:, :, :, 2 * pair : 2 * pair + 2],
+            )
+
+        def weight_tiles(label):
             codes = keep.tile([P, PASS], U32, name=label + "_q", align_bytes=64)
             scales = keep.tile([P, PASS], U8, name=label + "_s", align_bytes=64)
-            for engine, t0, t1 in shares:
-                nt = t1 - t0
-                if engine == "vector" and nt == 2:
-                    grouped = keep.tile([P, nt * PASS], BF16, name="w_first", tag="w_first", align_bytes=64)
-                else:
-                    grouped = ring.tile([P, nt * PASS], BF16, name="w_grouped", tag="w_grouped", bufs=3, align_bytes=64)
-                copy_on(
-                    engine,
-                    grouped[:].rearrange("p (t m j) -> p m j t", t=nt, j=PACK),
-                    raw[:].rearrange("p j (m t) -> p m j t", t=PACK)[:, :, :, t0:t1],
-                )
-                nc.vector.quantize_mx(
-                    out=codes[:, t0 * P : t1 * P].bitcast(FP8X4), scales=scales[:, t0 * P : t1 * P], in_=grouped[:]
-                )
+            grouped = ring.tile([P, PACK * PASS], BF16, name="w_grouped", tag="w_grouped", bufs=3, align_bytes=64)
+            return codes, scales, grouped
+
+        def quantise_weight(raw, label, engine):
+            codes, scales, grouped = weight_tiles(label)
+            for pair in range(2):
+                round_pair(engine, grouped, raw, pair)
+            nc.vector.quantize_mx(out=codes[:].bitcast(FP8X4), scales=scales[:], in_=grouped[:])
             return codes, scales
 
-        on_scalar = [("scalar", 0, 4)]
-        on_vector = [("vector", 0, 4)]
-        on_both = [("vector", 0, 2), ("scalar", 2, 4)]
+        def quantise_weight_shared(raw, label):
+            codes, scales, grouped = weight_tiles(label)
+            for pair, engine in enumerate(("scalar", "vector")):
+                round_pair(engine, grouped, raw, pair)
+                cols = slice(2 * pair * P, 2 * (pair + 1) * P)
+                nc.vector.quantize_mx(
+                    out=codes[:, cols].bitcast(FP8X4), scales=scales[:, cols],
+                    in_=grouped[:, 2 * pair * PASS : 2 * (pair + 1) * PASS],
+                )
+            return codes, scales
 
         w1_q = {}
         gather_table(0, 0)
         gather_table(0, 1)
-        load_later()
+        load_later_operands()
         deal_w2_words(0)
         deal_w2_words(1)
         deal_weight_scales(0)
-        w1_q[0, 0] = quantise_weight(w1_raw[0, 0], "w1_00", on_scalar)
+        w1_q[0, 0] = quantise_weight(w1_raw[0, 0], "w1_00", "scalar")
         deal_weight_scales(1)
         gather_table(1, 0)
         gather_table(1, 1)
-        w1_q[1, 0] = quantise_weight(w1_raw[1, 0], "w1_10", on_both)
+        w1_q[1, 0] = quantise_weight_shared(w1_raw[1, 0], "w1_10")
 
         def mm_w1(acc, a, b, t, half):
             codes, scales = w1_q[a, b]
-            cols = slice(t * P, (t + 1) * P)
+            places = slice(t * P, (t + 1) * P)
             nc.tensor.matmul_mx(
-                out=acc[:], lhsT=codes[:, cols].bitcast(FP8X4), lhsT_scale=scales[:, cols],
-                rhs=v_q[a, half][:].bitcast(FP8X4), rhs_scale=v_s[a][:, half * PASS : (half + 1) * PASS], start=(a == 0), stop=(a == 1),
+                out=acc[:], lhsT=codes[:, places].bitcast(FP8X4), lhsT_scale=scales[:, places],
+                rhs=v_q[a, half][:].bitcast(FP8X4), rhs_scale=v_s[a][:, half * PASS : (half + 1) * PASS],
+                start=(a == 0), stop=(a == 1),
             )
 
         def mm_w2(acc, a, b, t, half):
-            cols = slice(a * PASS + t * P, a * PASS + (t + 1) * P)
+            places = slice(a * PASS + t * P, a * PASS + (t + 1) * P)
             nc.tensor.matmul_mx(
-                out=acc[:], lhsT=w2_q[b][:, cols].bitcast(FP4X4), lhsT_scale=w2_s[b][:, cols],
-                rhs=v_q[a, half][:].bitcast(FP8X4),
-                rhs_scale=v_s[a][:, half * PASS : (half + 1) * PASS], start=(a == 0), stop=(a == 1),
+                out=acc[:], lhsT=w2_q[b][:, places].bitcast(FP4X4), lhsT_scale=weight_s[b][:, places],
+                rhs=v_q[a, half][:].bitcast(FP8X4), rhs_scale=v_s[a][:, half * PASS : (half + 1) * PASS],
+                start=(a == 0), stop=(a == 1),
             )
 
+        h_rows = {}
         h_q = {}
 
-        h_planes = {}
-
-        def first_stage(b, half, pass_major):
-            lin = [psum.tile([P, PASS], F32, name="lin", tag="acc") for t in range(PACK)] if pass_major else {}
-            proj = [psum.tile([P, PASS], F32, name="proj", tag="acc") for t in range(PACK)] if pass_major else {}
-            if pass_major:
-                for t in range(PACK):
-                    mm_w2(lin[t], 0, b, t, half)
-                for t in range(PACK):
-                    mm_w1(proj[t], 0, b, t, half)
-                for t in range(PACK):
-                    mm_w1(proj[t], 1, b, t, half)
-                    mm_w2(lin[t], 1, b, t, half)
-            planes = keep.tile([P, PACK, PASS], BF16, name="h_planes%d%d" % (b, half), align_bytes=64)
-            h_planes[b, half] = planes
-            for t in range(PACK):
-                if not pass_major:
-                    proj[t] = psum.tile([P, PASS], F32, name="proj", tag="acc")
-                    for a in range(2):
-                        mm_w1(proj[t], a, b, t, half)
-                    lin[t] = psum.tile([P, PASS], F32, name="lin", tag="acc")
-                    for a in range(2):
-                        mm_w2(lin[t], a, b, t, half)
-                away = ring.tile([P, PASS], F32, name="away", tag="away", bufs=4)
-                nc.scalar.activation(
-                    out=away[:], in_=proj[t][:], func=ACT.Abs, bias=cen_sb[:, b, t : t + 1], scale=-1.0
-                )
-                nc.vector.scalar_tensor_tensor(
-                    out=planes[:, t, :], in0=away[:], scalar=gain_sb[:, b, t : t + 1], in1=lin[t][:],
-                    op0=ALU.mult, op1=ALU.add,
-                )
-
-        def quantise_h(b, half, weave_engine):
-            planes = h_planes[b, half]
-            woven = ring.tile([P, PACK * PASS], BF16, name="h_woven", tag="h_woven", align_bytes=64)
-            copy_on(
-                weave_engine,
-                woven[:].rearrange("p (c i t) -> p c t i", i=4, t=PACK),
-                planes[:].rearrange("p t (c i) -> p c t i", i=4),
+        def combine(b, half, t, proj, lin):
+            away = ring.tile([P, PASS], F32, name="away", tag="away", bufs=PACK)
+            nc.scalar.activation(out=away[:], in_=proj[:], func=ACT.Abs, bias=cen_sb[:, b, t : t + 1], scale=-1.0)
+            nc.vector.scalar_tensor_tensor(
+                out=h_rows[b, half][:, t, :], in0=away[:], scalar=gain_sb[:, b, t : t + 1], in1=lin[:],
+                op0=ALU.mult, op1=ALU.add,
             )
+
+        def h_rows_tile(b, half):
+            h_rows[b, half] = keep.tile([P, PACK, PASS], BF16, name="h_rows%d%d" % (b, half), align_bytes=64)
+
+        def first_unit():
+            lin = [psum.tile([P, PASS], F32, name="lin", tag="acc") for t in range(PACK)]
+            proj = [psum.tile([P, PASS], F32, name="proj", tag="acc") for t in range(PACK)]
+            for t in range(PACK):
+                mm_w2(lin[t], 0, 0, t, 0)
+            for t in range(PACK):
+                mm_w1(proj[t], 0, 0, t, 0)
+            for t in range(PACK):
+                mm_w1(proj[t], 1, 0, t, 0)
+                mm_w2(lin[t], 1, 0, t, 0)
+            h_rows_tile(0, 0)
+            for t in range(PACK):
+                combine(0, 0, t, proj[t], lin[t])
+
+        def later_unit(b, half):
+            h_rows_tile(b, half)
+            for t in range(PACK):
+                proj = psum.tile([P, PASS], F32, name="proj", tag="acc")
+                for a in range(2):
+                    mm_w1(proj, a, b, t, half)
+                lin = psum.tile([P, PASS], F32, name="lin", tag="acc")
+                for a in range(2):
+                    mm_w2(lin, a, b, t, half)
+                combine(b, half, t, proj, lin)
+
+        def weave(engine, woven, rows):
+            copy_on(
+                engine,
+                woven.rearrange("p (c i t) -> p c t i", i=RUN, t=PACK),
+                rows.rearrange("p t (c i) -> p c t i", i=RUN),
+            )
+
+        def quantise_h(b, half, engine):
+            woven = ring.tile([P, PACK * PASS], BF16, name="h_woven", tag="h_woven", align_bytes=64)
+            weave(engine, woven[:], h_rows[b, half][:])
             codes = keep.tile([P, PASS], U32, name="h_q%d%d" % (b, half), align_bytes=64)
             scales = keep.tile([P, PASS], U8, name="h_s%d%d" % (b, half), align_bytes=64)
             nc.vector.quantize_mx(out=codes[:].bitcast(FP8X4), scales=scales[:], in_=woven[:])
             h_q[b, half] = (codes, scales)
 
-        wb_s = [w2_s[1][4:P, a * N : (a + 1) * N] for a in range(2)]
         neg_temp = keep.tile([P, PACK], F32, name="neg_temp")
         wa_q = {}
-        first_stage(0, 0, True)
-        w1_q[0, 1] = quantise_weight(w1_raw[0, 1], "w1_01", on_vector)
-        w1_q[1, 1] = quantise_weight(w1_raw[1, 1], "w1_11", on_scalar)
-        first_stage(0, 1, False)
+        first_unit()
+        w1_q[0, 1] = quantise_weight(w1_raw[0, 1], "w1_01", "vector")
+        w1_q[1, 1] = quantise_weight(w1_raw[1, 1], "w1_11", "scalar")
+        later_unit(0, 1)
         quantise_h(0, 0, "vector")
-        first_stage(1, 0, False)
-        wa_q[0] = quantise_weight(wa_raw[0], "wa_0", on_scalar)
+        later_unit(1, 0)
+        wa_q[0] = quantise_weight(wa_raw[0], "wa_0", "scalar")
         quantise_h(1, 0, "vector")
-        wa_q[1] = quantise_weight(wa_raw[1], "wa_1", on_scalar)
-        wb_q = keep.tile([P, 2 * N], U32, name="wb_q", align_bytes=64)
-        nc.scalar.copy(out=dealt(wb_q[:]), in_=undealt(wb_raw[:]))
+        wa_q[1] = quantise_weight(wa_raw[1], "wa_1", "scalar")
+        wb_words_q = keep.tile([P, 2 * N], U32, name="wb_words_q", align_bytes=64)
+        nc.scalar.copy(
+            out=wb_words_q[:].rearrange("p (b t m) -> p b m t", b=2, t=PACK),
+            in_=wb_raw[:].rearrange("p (b m t) -> p b m t", b=2, t=PACK),
+        )
         nc.vector.tensor_scalar(
             out=neg_temp[:], in0=temp_sb[:], scalar1=-1.0, scalar2=0.0, op0=ALU.mult, op1=ALU.add
         )
-        first_stage(1, 1, False)
+        later_unit(1, 1)
         quantise_h(0, 1, "scalar")
         quantise_h(1, 1, "vector")
 
@@ -285,19 +301,19 @@ def tile_list_streak_linkage_features_kernel(
         y_sb = keep.tile([P, PACK, NPICK], F32, name="y_sb")
         out_rows = out_0.rearrange("(p t) m -> p t m", t=PACK)
 
-        def second_product(weights, t, half):
+        def second_product(weight_q, t, half):
             acc = psum.tile([P, PASS], F32, name="acc2", tag="acc")
-            cols = slice(t * P, (t + 1) * P)
+            places = slice(t * P, (t + 1) * P)
             for b in range(2):
-                codes, scales = weights[b]
+                codes, scales = weight_q[b]
                 nc.tensor.matmul_mx(
-                    out=acc[:], lhsT=codes[:, cols].bitcast(FP8X4), lhsT_scale=scales[:, cols],
+                    out=acc[:], lhsT=codes[:, places].bitcast(FP8X4), lhsT_scale=scales[:, places],
                     rhs=h_q[b, half][0][:].bitcast(FP8X4), rhs_scale=h_q[b, half][1][:],
                     start=(b == 0), stop=(b == 1),
                 )
             return acc
 
-        wb_pair = [(wb_q[:, a * N : (a + 1) * N], wb_s[a]) for a in range(2)]
+        wb_q = [(wb_words_q[:, b * N : (b + 1) * N], weight_s[1][LIVE:P, b * N : (b + 1) * N]) for b in range(2)]
         for half in range(2):
             cols = slice(half * PASS, (half + 1) * PASS)
             for t in range(PACK):
@@ -307,23 +323,23 @@ def tile_list_streak_linkage_features_kernel(
                     scalar2=(None if half == 0 else top[0][:, t : t + 1]),
                     op0=ALU.mult, op1=ALU.max, accum_out=top[half][:, t : t + 1],
                 )
-                acc_d = second_product(wb_pair, t, half)
+                acc_d = second_product(wb_q, t, half)
                 nc.scalar.copy(out=d_sb[t][:, cols], in_=acc_d[:])
 
         for t in range(PACK):
             nc.scalar.activation(
                 out=shift[:, t : t + 1], in_=top[1][:, t : t + 1], func=ACT.Copy, scale=neg_temp[:, t : t + 1]
             )
-            weight = ring.tile([P, NPICK], F32, name="weight", tag="weight", bufs=4)
+            closeness = ring.tile([P, NPICK], F32, name="closeness", tag="closeness", bufs=PACK)
             nc.scalar.activation(
-                out=weight[:], in_=e_sb[t][:].indirect(pos1_sb[:]), func=ACT.Exp,
+                out=closeness[:], in_=e_sb[t][:].indirect(pos1_sb[:]), func=ACT.Exp,
                 bias=shift[:, t : t + 1], scale=temp_sb[:, t : t + 1],
             )
-            mixed = ring.tile([P, NPICK], F32, name="mixed", tag="mixed", bufs=4)
+            mixed = ring.tile([P, NPICK], F32, name="mixed", tag="mixed", bufs=PACK)
             nc.vector.tensor_tensor(
                 out=mixed[:], in0=d_sb[t][:].indirect(pos2_sb[:]), in1=mix_sb[:, t, :], op=ALU.mult
             )
-            nc.vector.tensor_tensor(out=y_sb[:, t, :], in0=weight[:], in1=mixed[:], op=ALU.mult)
+            nc.vector.tensor_tensor(out=y_sb[:, t, :], in0=closeness[:], in1=mixed[:], op=ALU.mult)
             nc.sync.dma_start(out=out_rows[:, t, :], in_=y_sb[:, t, :])
 
         y_q = keep.tile([P, NPICK], U32, name="y_q", align_bytes=64)
@@ -332,17 +348,14 @@ def tile_list_streak_linkage_features_kernel(
         for part, engine in enumerate(("vector", "scalar")):
             cols = slice(part * width, (part + 1) * width)
             y_woven = ring.tile([P, PACK * width], BF16, name="y_woven", tag="y_woven", align_bytes=64)
-            copy_on(
-                engine,
-                y_woven[:].rearrange("p (c i t) -> p c t i", i=4, t=PACK),
-                y_sb[:, :, cols].rearrange("p t (c i) -> p c t i", i=4),
-            )
+            weave(engine, y_woven[:], y_sb[:, :, cols])
             nc.vector.quantize_mx(out=y_q[:, cols].bitcast(FP8X4), scales=y_s[:, cols], in_=y_woven[:])
-        nc.sync.dma_start(
-            out=out_1[0].rearrange("p m i -> p (m i)").bitcast(I32), in_=y_q[:].bitcast(I32)
-        )
+            nc.sync.dma_start(
+                out=out_1[0].rearrange("p m i -> p (m i)").bitcast(I32)[:, cols], in_=y_q[:, cols].bitcast(I32)
+            )
         for q in range(QUADS):
             queue = nc.sync if q % 2 == 0 else nc.scalar
             queue.dma_start(
-                out=out_2[0, 4 * q : 4 * q + 4, :].bitcast(I32), in_=y_s[32 * q : 32 * q + 4, :].bitcast(I32)
+                out=out_2[0, LIVE * q : LIVE * (q + 1), :].bitcast(I32),
+                in_=y_s[QUAD * q : QUAD * q + LIVE, :].bitcast(I32),
             )

from contextlib import ExitStack

import concourse.mybir as mybir

K, T, S, NPICK, H, N = 1024, 2048, 1024, 512, 1024, 512
FLOPS = 2 * (2 * K * H * S + 2 * H * N * S)

F32 = mybir.dt.float32
BF16 = mybir.dt.bfloat16
I32 = mybir.dt.int32
U32 = mybir.dt.uint32
U16 = mybir.dt.uint16
U8 = mybir.dt.uint8
FP8X4 = mybir.dt.float8_e4m3fn_x4
FP4X4 = mybir.dt.float4_e2m1fn_x4
ALU = mybir.AluOpType
ACT = mybir.ActivationFunctionType

P = 128
PACK = 4
PASS = P * PACK
QUADS = 4
QUAD = P // QUADS
LIVE = 4
LIST_GROUP = 16
SPREAD = 4
RUN = 4


def tile_list_streak_linkage_features_kernel(
    tc, tab_words, tab_scales, offs, pos1, pos2, w1, cen, gain, w2_words, w2_scales,
    wa, wb_words, wb_scales, temp, mix, out_0, out_1, out_2,
):
    nc = tc.nc

    def copy_on(engine, out, in_):
        if engine == "scalar":
            nc.scalar.copy(out=out, in_=in_)
        else:
            nc.vector.tensor_copy(out=out, in_=in_)

    with ExitStack() as ctx:
        keep = ctx.enter_context(tc.tile_pool(name="keep", bufs=1))
        ring = ctx.enter_context(tc.tile_pool(name="ring", bufs=2))
        staged = ctx.enter_context(tc.tile_pool(name="staged", bufs=3))
        psum = ctx.enter_context(tc.psum_pool(name="psum", bufs=8))

        offs_sb = keep.tile([P, S // LIST_GROUP], U16, name="offs_sb")
        pos1_sb = keep.tile([P, NPICK // LIST_GROUP], U16, name="pos1_sb")
        pos2_sb = keep.tile([P, NPICK // LIST_GROUP], U16, name="pos2_sb")
        tab_w = [keep.tile([P, T], U32, name="tab_w%d" % a, align_bytes=64) for a in range(2)]
        tab_s = keep.tile([P, T], U8, name="tab_s", align_bytes=64)
        w2_raw = staged.tile([P, 2 * H], U16, name="w2_raw", tag="raw")
        weight_s_raw = keep.tile([P, 2 * H], U8, name="weight_s_raw", align_bytes=64)
        w1_raw = {
            (a, b): staged.tile([P, PACK, PASS], F32, name="w1_raw%d%d" % (a, b), tag="raw")
            for b in range(2) for a in range(2)
        }
        wa_raw = [staged.tile([P, PACK, N], F32, name="wa_raw%d" % b, tag="raw") for b in range(2)]
        wb_raw = staged.tile([P, 2 * N], U32, name="wb_raw", tag="raw")
        cen_sb = keep.tile([P, 2, PACK], F32, name="cen_sb")
        gain_sb = keep.tile([P, 2, PACK], F32, name="gain_sb")
        temp_sb = keep.tile([P, PACK], F32, name="temp_sb")
        mix_sb = staged.tile([P, PACK, NPICK], F32, name="mix_sb", tag="raw")

        nc.gpsimd.memset(tab_s[:].bitcast(I32), 0)
        nc.vector.memset(weight_s_raw[:].bitcast(I32), 0)
        v_s = [keep.tile([P, S], U8, name="v_s%d" % a, align_bytes=64) for a in range(2)]
        for a in range(2):
            nc.vector.memset(v_s[a][:].bitcast(I32), 0)
        picked_s = keep.tile([P, S], U8, name="picked_s", align_bytes=64)

        def load_weight_scales(scales, row, first_byte):
            width = scales.shape[2]
            for q in range(QUADS):
                rows = weight_s_raw[QUAD * q + row : QUAD * q + row + LIVE, :].bitcast(I32)
                nc.sync.dma_start(
                    out=rows.rearrange("r (g c) -> r g c", g=2)[:, :, first_byte // 4 : (first_byte + width) // 4],
                    in_=scales[:, LIVE * q : LIVE * (q + 1), :].bitcast(I32).rearrange("g r c -> r g c"),
                )

        def load_tab_words(a):
            nc.sync.dma_start(
                out=tab_w[a][:].bitcast(I32), in_=tab_words[a].rearrange("p c i -> p (c i)").bitcast(I32)
            )

        def load_rows(raw, rows):
            nc.sync.dma_start(out=raw[:], in_=rows.rearrange("(p j) c -> p j c", j=PACK))

        def load_w1(a, b):
            load_rows(w1_raw[a, b], w1[a * PASS : (a + 1) * PASS, b * PASS : (b + 1) * PASS])

        def move_table_scales(a):
            for q in range(QUADS):
                first = SPREAD * LIVE * (QUADS * a + q)
                nc.sync.dma_start(
                    out=v_s[a][QUAD * q : QUAD * q + LIVE, :].bitcast(I32),
                    in_=picked_s[first : first + SPREAD * LIVE : SPREAD, :].bitcast(I32),
                )

        nc.sync.dma_start(offs_sb[:], offs)
        nc.sync.dma_start(
            out=w2_raw[:].bitcast(I32).rearrange("p (a c) -> p a c", a=2),
            in_=w2_words.bitcast(I32).rearrange("a p c -> p a c"),
        )
        nc.sync.dma_start(
            out=tab_s[0:P:SPREAD, :].bitcast(I32), in_=tab_scales.rearrange("a i c -> (a i) c").bitcast(I32)
        )
        nc.vector.tensor_copy(out=picked_s[:], in_=tab_s[:].indirect(offs_sb[:]))
        load_tab_words(0)
        load_weight_scales(w2_scales, 0, 0)
        load_w1(0, 0)
        load_weight_scales(wb_scales, LIVE, PASS)
        load_tab_words(1)
        move_table_scales(0)
        load_w1(1, 0)
        move_table_scales(1)
        nc.gpsimd.dma_start(out=cen_sb[:], in_=cen.rearrange("(b p t) -> p b t", b=2, t=PACK))
        nc.gpsimd.dma_start(out=gain_sb[:], in_=gain.rearrange("(b p t) -> p b t", b=2, t=PACK))

        def load_later_operands():
            load_w1(0, 1)
            load_w1(1, 1)
            for b in range(2):
                load_rows(wa_raw[b], wa[b * PASS : (b + 1) * PASS, :])
            nc.sync.dma_start(
                out=wb_raw[:].bitcast(I32).rearrange("p (b c) -> p b c", b=2),
                in_=wb_words.rearrange("b p c i -> b p (c i)").bitcast(I32).rearrange("b p c -> p b c"),
            )
            load_rows(mix_sb, mix)
            nc.sync.dma_start(pos1_sb[:], pos1)
            nc.sync.dma_start(pos2_sb[:], pos2)
            nc.sync.dma_start(out=temp_sb[:], in_=temp.rearrange("(p t) -> p t", t=PACK))

        w2_q = [keep.tile([P, H], U16, name="w2_q%d" % b, align_bytes=64) for b in range(2)]
        weight_s = [keep.tile([P, H], U8, name="weight_s%d" % b, align_bytes=64) for b in range(2)]

        def block_of(raw, b):
            return raw[:].rearrange("p (a b m t) -> p a b t m", a=2, b=2, t=PACK)[:, :, b, :, :]

        def places_of(dealt):
            return dealt[:].rearrange("p (a t m) -> p a t m", a=2, t=PACK)

        def deal_w2_words(b):
            nc.scalar.copy(out=places_of(w2_q[b]), in_=block_of(w2_raw, b))

        def deal_weight_scales(b):
            nc.vector.tensor_copy(out=places_of(weight_s[b]), in_=block_of(weight_s_raw, b))

        v_q = {}

        def gather_table(a, half):
            cols = PASS // LIST_GROUP
            v_q[a, half] = keep.tile([P, PASS], U32, name="v_q%d%d" % (a, half), align_bytes=64)
            nc.vector.tensor_copy(
                out=v_q[a, half][:], in_=tab_w[a][:].indirect(offs_sb[:, half * cols : (half + 1) * cols])
            )

        def round_pair(engine, grouped, raw, pair):
            copy_on(
                engine,
                grouped[:, 2 * pair * PASS : 2 * (pair + 1) * PASS].rearrange("p (t m j) -> p m j t", t=2, j=PACK),
                raw[:].rearrange("p j (m t) -> p m j t", t=PACK)[:, :, :, 2 * pair : 2 * pair + 2],
            )

        def weight_tiles(label):
            codes = keep.tile([P, PASS], U32, name=label + "_q", align_bytes=64)
            scales = keep.tile([P, PASS], U8, name=label + "_s", align_bytes=64)
            grouped = ring.tile([P, PACK * PASS], BF16, name="w_grouped", tag="w_grouped", bufs=3, align_bytes=64)
            return codes, scales, grouped

        def quantise_weight(raw, label, engine):
            codes, scales, grouped = weight_tiles(label)
            for pair in range(2):
                round_pair(engine, grouped, raw, pair)
            nc.vector.quantize_mx(out=codes[:].bitcast(FP8X4), scales=scales[:], in_=grouped[:])
            return codes, scales

        def quantise_weight_shared(raw, label):
            codes, scales, grouped = weight_tiles(label)
            for pair, engine in enumerate(("scalar", "vector")):
                round_pair(engine, grouped, raw, pair)
                cols = slice(2 * pair * P, 2 * (pair + 1) * P)
                nc.vector.quantize_mx(
                    out=codes[:, cols].bitcast(FP8X4), scales=scales[:, cols],
                    in_=grouped[:, 2 * pair * PASS : 2 * (pair + 1) * PASS],
                )
            return codes, scales

        w1_q = {}
        gather_table(0, 0)
        gather_table(0, 1)
        load_later_operands()
        deal_w2_words(0)
        deal_w2_words(1)
        deal_weight_scales(0)
        w1_q[0, 0] = quantise_weight(w1_raw[0, 0], "w1_00", "scalar")
        deal_weight_scales(1)
        gather_table(1, 0)
        gather_table(1, 1)
        w1_q[1, 0] = quantise_weight_shared(w1_raw[1, 0], "w1_10")

        def mm_w1(acc, a, b, t, half):
            codes, scales = w1_q[a, b]
            places = slice(t * P, (t + 1) * P)
            nc.tensor.matmul_mx(
                out=acc[:], lhsT=codes[:, places].bitcast(FP8X4), lhsT_scale=scales[:, places],
                rhs=v_q[a, half][:].bitcast(FP8X4), rhs_scale=v_s[a][:, half * PASS : (half + 1) * PASS],
                start=(a == 0), stop=(a == 1),
            )

        def mm_w2(acc, a, b, t, half):
            places = slice(a * PASS + t * P, a * PASS + (t + 1) * P)
            nc.tensor.matmul_mx(
                out=acc[:], lhsT=w2_q[b][:, places].bitcast(FP4X4), lhsT_scale=weight_s[b][:, places],
                rhs=v_q[a, half][:].bitcast(FP8X4), rhs_scale=v_s[a][:, half * PASS : (half + 1) * PASS],
                start=(a == 0), stop=(a == 1),
            )

        h_rows = {}
        h_q = {}

        def combine(b, half, t, proj, lin):
            away = ring.tile([P, PASS], F32, name="away", tag="away", bufs=PACK)
            nc.scalar.activation(out=away[:], in_=proj[:], func=ACT.Abs, bias=cen_sb[:, b, t : t + 1], scale=-1.0)
            nc.vector.scalar_tensor_tensor(
                out=h_rows[b, half][:, t, :], in0=away[:], scalar=gain_sb[:, b, t : t + 1], in1=lin[:],
                op0=ALU.mult, op1=ALU.add,
            )

        def h_rows_tile(b, half):
            h_rows[b, half] = keep.tile([P, PACK, PASS], BF16, name="h_rows%d%d" % (b, half), align_bytes=64)

        def first_unit():
            lin = [psum.tile([P, PASS], F32, name="lin", tag="acc") for t in range(PACK)]
            proj = [psum.tile([P, PASS], F32, name="proj", tag="acc") for t in range(PACK)]
            for t in range(PACK):
                mm_w2(lin[t], 0, 0, t, 0)
            for t in range(PACK):
                mm_w1(proj[t], 0, 0, t, 0)
            for t in range(PACK):
                mm_w1(proj[t], 1, 0, t, 0)
                mm_w2(lin[t], 1, 0, t, 0)
            h_rows_tile(0, 0)
            for t in range(PACK):
                combine(0, 0, t, proj[t], lin[t])

        def later_unit(b, half):
            h_rows_tile(b, half)
            for t in range(PACK):
                proj = psum.tile([P, PASS], F32, name="proj", tag="acc")
                for a in range(2):
                    mm_w1(proj, a, b, t, half)
                lin = psum.tile([P, PASS], F32, name="lin", tag="acc")
                for a in range(2):
                    mm_w2(lin, a, b, t, half)
                combine(b, half, t, proj, lin)

        def weave(engine, woven, rows):
            copy_on(
                engine,
                woven.rearrange("p (c i t) -> p c t i", i=RUN, t=PACK),
                rows.rearrange("p t (c i) -> p c t i", i=RUN),
            )

        def quantise_h(b, half, engine):
            woven = ring.tile([P, PACK * PASS], BF16, name="h_woven", tag="h_woven", align_bytes=64)
            weave(engine, woven[:], h_rows[b, half][:])
            codes = keep.tile([P, PASS], U32, name="h_q%d%d" % (b, half), align_bytes=64)
            scales = keep.tile([P, PASS], U8, name="h_s%d%d" % (b, half), align_bytes=64)
            nc.vector.quantize_mx(out=codes[:].bitcast(FP8X4), scales=scales[:], in_=woven[:])
            h_q[b, half] = (codes, scales)

        neg_temp = keep.tile([P, PACK], F32, name="neg_temp")
        wa_q = {}
        first_unit()
        w1_q[0, 1] = quantise_weight(w1_raw[0, 1], "w1_01", "vector")
        w1_q[1, 1] = quantise_weight(w1_raw[1, 1], "w1_11", "scalar")
        later_unit(0, 1)
        quantise_h(0, 0, "vector")
        later_unit(1, 0)
        wa_q[0] = quantise_weight(wa_raw[0], "wa_0", "scalar")
        quantise_h(1, 0, "vector")
        wa_q[1] = quantise_weight(wa_raw[1], "wa_1", "scalar")
        wb_words_q = keep.tile([P, 2 * N], U32, name="wb_words_q", align_bytes=64)
        nc.scalar.copy(
            out=wb_words_q[:].rearrange("p (b t m) -> p b m t", b=2, t=PACK),
            in_=wb_raw[:].rearrange("p (b m t) -> p b m t", b=2, t=PACK),
        )
        nc.vector.tensor_scalar(
            out=neg_temp[:], in0=temp_sb[:], scalar1=-1.0, scalar2=0.0, op0=ALU.mult, op1=ALU.add
        )
        later_unit(1, 1)
        quantise_h(0, 1, "scalar")
        quantise_h(1, 1, "vector")

        e_sb = [keep.tile([P, S], F32, name="e_sb%d" % t) for t in range(PACK)]
        d_sb = [keep.tile([P, S], F32, name="d_sb%d" % t) for t in range(PACK)]
        top = [keep.tile([P, PACK], F32, name="top%d" % half) for half in range(2)]
        shift = keep.tile([P, PACK], F32, name="shift")
        y_sb = keep.tile([P, PACK, NPICK], F32, name="y_sb")
        out_rows = out_0.rearrange("(p t) m -> p t m", t=PACK)

        def second_product(weight_q, t, half):
            acc = psum.tile([P, PASS], F32, name="acc2", tag="acc")
            places = slice(t * P, (t + 1) * P)
            for b in range(2):
                codes, scales = weight_q[b]
                nc.tensor.matmul_mx(
                    out=acc[:], lhsT=codes[:, places].bitcast(FP8X4), lhsT_scale=scales[:, places],
                    rhs=h_q[b, half][0][:].bitcast(FP8X4), rhs_scale=h_q[b, half][1][:],
                    start=(b == 0), stop=(b == 1),
                )
            return acc

        wb_q = [(wb_words_q[:, b * N : (b + 1) * N], weight_s[1][LIVE:P, b * N : (b + 1) * N]) for b in range(2)]
        for half in range(2):
            cols = slice(half * PASS, (half + 1) * PASS)
            for t in range(PACK):
                acc_e = second_product(wa_q, t, half)
                nc.vector.tensor_scalar(
                    out=e_sb[t][:, cols], in0=acc_e[:], scalar1=1.0,
                    scalar2=(None if half == 0 else top[0][:, t : t + 1]),
                    op0=ALU.mult, op1=ALU.max, accum_out=top[half][:, t : t + 1],
                )
                acc_d = second_product(wb_q, t, half)
                nc.scalar.copy(out=d_sb[t][:, cols], in_=acc_d[:])

        for t in range(PACK):
            nc.scalar.activation(
                out=shift[:, t : t + 1], in_=top[1][:, t : t + 1], func=ACT.Copy, scale=neg_temp[:, t : t + 1]
            )
            closeness = ring.tile([P, NPICK], F32, name="closeness", tag="closeness", bufs=PACK)
            nc.scalar.activation(
                out=closeness[:], in_=e_sb[t][:].indirect(pos1_sb[:]), func=ACT.Exp,
                bias=shift[:, t : t + 1], scale=temp_sb[:, t : t + 1],
            )
            mixed = ring.tile([P, NPICK], F32, name="mixed", tag="mixed", bufs=PACK)
            nc.vector.tensor_tensor(
                out=mixed[:], in0=d_sb[t][:].indirect(pos2_sb[:]), in1=mix_sb[:, t, :], op=ALU.mult
            )
            nc.vector.tensor_tensor(out=y_sb[:, t, :], in0=closeness[:], in1=mixed[:], op=ALU.mult)
            nc.sync.dma_start(out=out_rows[:, t, :], in_=y_sb[:, t, :])

        y_q = keep.tile([P, NPICK], U32, name="y_q", align_bytes=64)
        y_s = keep.tile([P, NPICK], U8, name="y_s", align_bytes=64)
        width = NPICK // 2
        for part, engine in enumerate(("vector", "scalar")):
            cols = slice(part * width, (part + 1) * width)
            y_woven = ring.tile([P, PACK * width], BF16, name="y_woven", tag="y_woven", align_bytes=64)
            weave(engine, y_woven[:], y_sb[:, :, cols])
            nc.vector.quantize_mx(out=y_q[:, cols].bitcast(FP8X4), scales=y_s[:, cols], in_=y_woven[:])
            nc.sync.dma_start(
                out=out_1[0].rearrange("p m i -> p (m i)").bitcast(I32)[:, cols], in_=y_q[:, cols].bitcast(I32)
            )
        for q in range(QUADS):
            queue = nc.sync if q % 2 == 0 else nc.scalar
            queue.dma_start(
                out=out_2[0, LIVE * q : LIVE * (q + 1), :].bitcast(I32),
                in_=y_s[QUAD * q : QUAD * q + LIVE, :].bitcast(I32),
            )
